import numpy as np
import ml_dtypes


def mxq(x, axis, fmt="e4m3"):
    dtype, down = {"e4m3": (ml_dtypes.float8_e4m3fn, 7), "e5m2": (ml_dtypes.float8_e5m2, 14)}[fmt]
    v = np.moveaxis(np.asarray(x, np.float32).astype(ml_dtypes.bfloat16).astype(np.float64), axis, -1)
    blocks = v.reshape(v.shape[:-1] + (-1, 32))
    amax = np.abs(blocks).max(-1, keepdims=True)
    byte = np.maximum(np.where(amax > 0, np.frexp(amax)[1] - 1 + 127, 0) - down, 1)
    scale = np.exp2(byte - 127.0)
    codes = (blocks / scale).astype(np.float32).astype(dtype).astype(np.float64)
    return np.moveaxis((codes * scale).reshape(v.shape), -1, axis)


WIDE = False


def mx_kscale(k, group=512):
    if not WIDE:
        return np.ones(k)
    levels = np.array([18, -18])
    if group != 512:
        return np.exp2(np.random.permutation(np.resize(levels, k // group))).repeat(group)
    if k % 512:
        return np.exp2(np.random.permutation(np.resize(levels, k // 32))).repeat(32)
    a = np.empty((k // 512, 16))
    for p in range(k // 512):
        a[p, :8] = np.random.permutation(np.resize(levels, 8))
        for g in range(8):
            far = levels[np.abs(levels - a[p, g]) >= 10]
            a[p, g + 8] = far[np.random.randint(len(far))]
    return np.exp2(a.ravel()).repeat(32)


def f64(x):
    return np.asarray(x).astype(np.float64)


G, D, E, O, N = 4, 128, 128, 256, 512


def sgn(shape):
    return np.random.uniform(0.5, 2.0, shape) * np.where(np.random.standard_normal(shape) < 0, -1.0, 1.0)


def setup_inputs():
    n = np.random.standard_normal
    s_d = mx_kscale(D, 0)
    s_ge = mx_kscale(G * E).reshape(G, E)
    return {
        "x": (n((G, D, N)) * s_d[:, None]).astype(np.float32),
        "w": (n((G, D, E)) / np.sqrt(D) / s_d[:, None]).astype(np.float32),
        "xb": (n((G, E, N))).astype(np.float32),
        "hs": (sgn((G, E, 1)) * s_ge[:, :, None]).astype(np.float32),
        "wo": (n((G, E, O)) / np.sqrt(G * E) / s_ge[:, :, None]).astype(np.float32),
        "bo": (0.5 * n((O, 1))).astype(np.float32),
    }


def reference(x, w, xb, hs, wo, bo):
    wq = mxq(f64(w), 1, "e4m3")
    xq = mxq(f64(x), 1, "e4m3")
    z = wq.transpose(0, 2, 1) @ xq
    h = z * f64(xb) * f64(hs)
    woq = mxq((f64(wo)).reshape(G * E, -1), 0, "e4m3")
    hq = mxq((h).reshape(G * E, -1), 0, "e4m3")
    u = woq.T @ hq
    y = np.tanh(u + f64(bo))
    return y

@@ -1,0 +1,149 @@
+from contextlib import ExitStack
+
+import concourse.mybir as mybir
+
+G, D, E, O, N = 4, 128, 128, 256, 512
+FLOPS = 2 * G * D * E * N + 2 * G * E * O * N
+
+F32 = mybir.dt.float32
+BF16 = mybir.dt.bfloat16
+U32 = mybir.dt.uint32
+U8 = mybir.dt.uint8
+FP8X4 = mybir.dt.float8_e4m3fn_x4
+ACT = mybir.ActivationFunctionType
+ALU = mybir.AluOpType
+
+P = 128
+PACK = 4
+ROWS = 32
+MM_N = 128
+CHUNK = 256
+
+
+def tile_rows_rnx_prod_kernel(tc, x, w, xb, hs, wo, bo, out):
+    nc = tc.nc
+    chunks = N // CHUNK
+    x_k = x.rearrange("g (p j) n -> (g p) j n", j=PACK)
+    w_k = w.rearrange("g (p j) e -> (g p) j e", j=PACK)
+    wo_k = wo.rearrange("g (p j) o -> (g p) j o", j=PACK)
+    xb_e = xb.rearrange("g e n -> e g n")
+    out_p = out.rearrange("(h p) n -> p h n", p=P)
+
+    with ExitStack() as ctx:
+        sb = ctx.enter_context(tc.tile_pool(name="sb", bufs=1))
+        ps = ctx.enter_context(tc.psum_pool(name="ps", bufs=1))
+        ctx.enter_context(tc.manual_schedule())
+
+        def tile(name, shape, dtype):
+            return sb.tile(shape, dtype, name=name, align_bytes=64)
+
+        def operand(name, width):
+            return (
+                tile(name + "_bf", [P, width, PACK], BF16),
+                tile(name + "_codes", [P, width], U32),
+                tile(name + "_scales", [P, width], U8),
+            )
+
+        def interleave(engine, dst, src, lo, hi):
+            view = src[:, :, lo:hi].rearrange("p j n -> p n j")
+            if engine == "scalar":
+                nc.scalar.copy(out=dst[:, lo:hi, :], in_=view)
+            else:
+                nc.vector.tensor_copy(out=dst[:, lo:hi, :], in_=view)
+
+        def quantize(op):
+            bf, codes, scales = op
+            nc.vector.quantize_mx(
+                out=codes[:].bitcast(FP8X4), scales=scales[:], in_=bf[:].rearrange("p n j -> p (n j)")
+            )
+
+        w_raw = tile("w_raw", [P, PACK, E], F32)
+        wo_raw = tile("wo_raw", [P, PACK, O], F32)
+        vec_rows = tile("vec_rows", [P, ROWS], F32)
+        vec = tile("vec", [P, ROWS], F32)
+        warm = tile("warm", [P, 1], F32)
+        x_raw = [tile("x_raw%d" % c, [P, PACK, CHUNK], F32) for c in range(chunks)]
+        xb_t = [tile("xb_t%d" % c, [P, G, CHUNK], F32) for c in range(chunks)]
+        h_e = [tile("h_e%d" % c, [P, G, CHUNK], BF16) for c in range(chunks)]
+        h_k = [tile("h_k%d" % c, [P, PACK, CHUNK], BF16) for c in range(chunks)]
+        y = [tile("y%d" % c, [P, O // P, CHUNK], F32) for c in range(chunks)]
+        w_op = operand("w", E)
+        wo_op = operand("wo", O)
+        x_op = [operand("x%d" % c, CHUNK) for c in range(chunks)]
+        h_op = [operand("h%d" % c, CHUNK) for c in range(chunks)]
+        z = [ps.tile([P, N], F32, name="z%d" % g) for g in range(G)]
+        u = [[ps.tile([P, CHUNK], F32, name="u%d_%d" % (c, h)) for h in range(O // P)] for c in range(chunks)]
+
+        def cols(c):
+            return slice(c * CHUNK, (c + 1) * CHUNK)
+
+        nc.sync.dma_start(out=w_raw[:], in_=w_k)
+        for c in range(chunks):
+            nc.sync.dma_start(out=x_raw[c][:], in_=x_k[:, :, cols(c)])
+            nc.sync.dma_start(out=xb_t[c][:], in_=xb_e[:, :, cols(c)])
+        nc.sync.dma_start(out=wo_raw[:], in_=wo_k)
+        nc.gpsimd.memset(vec_rows[:], 0.0)
+        nc.gpsimd.dma_start(out=vec_rows[0:P:8, :], in_=hs.rearrange("g (q i) o -> q g (i o)", i=ROWS))
+        nc.gpsimd.dma_start(out=vec_rows[1:P:16, :], in_=bo.rearrange("(h q i) o -> q h (i o)", h=O // P, i=ROWS))
+        nc.vector.memset(warm[:], 0.0)
+        nc.scalar.activation(out=warm[:], in_=warm[:], func=ACT.Tanh)
+
+        def first_product(c):
+            for n0 in range(0, CHUNK, MM_N):
+                for g in range(G):
+                    rows = slice(ROWS * g, ROWS * (g + 1))
+                    nc.tensor.matmul_mx(
+                        out=z[g][:, c * CHUNK + n0 : c * CHUNK + n0 + MM_N],
+                        lhsT=w_op[1][rows, :].bitcast(FP8X4),
+                        lhsT_scale=w_op[2][rows, :],
+                        rhs=x_op[c][1][rows, n0 : n0 + MM_N].bitcast(FP8X4),
+                        rhs_scale=x_op[c][2][rows, n0 : n0 + MM_N],
+                        start=True,
+                        stop=True,
+                    )
+
+        def fuse(c, g):
+            nc.vector.scalar_tensor_tensor(
+                out=h_e[c][:, g, :], in0=z[g][:, cols(c)], scalar=vec[:, 8 * g : 8 * g + 1], in1=xb_t[c][:, g, :],
+                op0=ALU.mult, op1=ALU.mult,
+            )
+            nc.sync.dma_start(out=h_k[c][ROWS * g : ROWS * (g + 1), :, :], in_=h_e[c][:, g, :])
+
+        def second_product(c):
+            for h in range(O // P):
+                for n0 in range(0, CHUNK, MM_N):
+                    nc.tensor.matmul_mx(
+                        out=u[c][h][:, n0 : n0 + MM_N],
+                        lhsT=wo_op[1][:, h * P : (h + 1) * P].bitcast(FP8X4),
+                        lhsT_scale=wo_op[2][:, h * P : (h + 1) * P],
+                        rhs=h_op[c][1][:, n0 : n0 + MM_N].bitcast(FP8X4),
+                        rhs_scale=h_op[c][2][:, n0 : n0 + MM_N],
+                        start=True,
+                        stop=True,
+                    )
+            for h in range(O // P):
+                nc.scalar.activation(out=y[c][:, h, :], in_=u[c][h][:], func=ACT.Tanh, bias=vec[:, 16 * h + 1 : 16 * h + 2])
+            nc.sync.dma_start(out=out_p[:, :, cols(c)], in_=y[c][:])
+
+        interleave("scalar", w_op[0], w_raw, 0, E)
+        nc.vector.transpose(out=vec[:], in_=vec_rows[:])
+        interleave("vector", x_op[0][0], x_raw[0], 0, 176)
+        interleave("scalar", x_op[0][0], x_raw[0], 176, CHUNK)
+        quantize(w_op)
+        quantize(x_op[0])
+        first_product(0)
+        interleave("scalar", x_op[1][0], x_raw[1], 96, CHUNK)
+        for g in (0, 2, 1, 3):
+            fuse(0, g)
+        interleave("vector", x_op[1][0], x_raw[1], 0, 96)
+        quantize(x_op[1])
+        first_product(1)
+        interleave("scalar", wo_op[0], wo_raw, 0, O)
+        for g in (0, 2, 1, 3):
+            fuse(1, g)
+        quantize(wo_op)
+        for c in range(chunks):
+            interleave("vector", h_op[c][0], h_k[c], 0, 176)
+            interleave("scalar", h_op[c][0], h_k[c], 176, CHUNK)
+            quantize(h_op[c])
+            second_product(c)

@@ -51,10 +51,12 @@ def tile_rows_rnx_prod_kernel(tc, x, w, xb, hs, wo, bo, out):
             else:
                 nc.vector.tensor_copy(out=dst[:, lo:hi, :], in_=view)
 
-        def quantize(op):
+        def quantize(op, lo, hi):
             bf, codes, scales = op
             nc.vector.quantize_mx(
-                out=codes[:].bitcast(FP8X4), scales=scales[:], in_=bf[:].rearrange("p n j -> p (n j)")
+                out=codes[:, lo:hi].bitcast(FP8X4),
+                scales=scales[:, lo:hi],
+                in_=bf[:, lo:hi, :].rearrange("p n j -> p (n j)"),
             )
 
         w_raw = tile("w_raw", [P, PACK, E], F32)
@@ -72,25 +74,27 @@ def tile_rows_rnx_prod_kernel(tc, x, w, xb, hs, wo, bo, out):
         x_op = [operand("x%d" % c, CHUNK) for c in range(chunks)]
         h_op = [operand("h%d" % c, CHUNK) for c in range(chunks)]
         z = [ps.tile([P, N], F32, name="z%d" % g) for g in range(G)]
-        u = [[ps.tile([P, CHUNK], F32, name="u%d_%d" % (c, h)) for h in range(O // P)] for c in range(chunks)]
+        u = [ps.tile([P, CHUNK], F32, name="u%d" % i) for i in range(4)]
 
         def cols(c):
             return slice(c * CHUNK, (c + 1) * CHUNK)
 
+        nc.vector.memset(vec_rows[:], 0.0)
         nc.sync.dma_start(out=w_raw[:], in_=w_k)
+        nc.sync.dma_start(out=x_raw[0][:], in_=x_k[:, :, cols(0)])
+        nc.sync.dma_start(out=vec_rows[0:P:8, :], in_=hs.rearrange("g (q i) o -> q g (i o)", i=ROWS))
+        nc.sync.dma_start(out=vec_rows[1:P:16, :], in_=bo.rearrange("(h q i) o -> q h (i o)", h=O // P, i=ROWS))
+        nc.sync.dma_start(out=x_raw[1][:], in_=x_k[:, :, cols(1)])
         for c in range(chunks):
-            nc.sync.dma_start(out=x_raw[c][:], in_=x_k[:, :, cols(c)])
-            nc.sync.dma_start(out=xb_t[c][:], in_=xb_e[:, :, cols(c)])
+            nc.sync.dma_start(out=xb_t[c][:, 0:2, :], in_=xb_e[:, 0:2, cols(c)])
+            nc.sync.dma_start(out=xb_t[c][:, 2:4, :], in_=xb_e[:, 2:4, cols(c)])
         nc.sync.dma_start(out=wo_raw[:], in_=wo_k)
-        nc.gpsimd.memset(vec_rows[:], 0.0)
-        nc.gpsimd.dma_start(out=vec_rows[0:P:8, :], in_=hs.rearrange("g (q i) o -> q g (i o)", i=ROWS))
-        nc.gpsimd.dma_start(out=vec_rows[1:P:16, :], in_=bo.rearrange("(h q i) o -> q h (i o)", h=O // P, i=ROWS))
         nc.vector.memset(warm[:], 0.0)
         nc.scalar.activation(out=warm[:], in_=warm[:], func=ACT.Tanh)
 
-        def first_product(c):
+        def first_product(c, groups):
             for n0 in range(0, CHUNK, MM_N):
-                for g in range(G):
+                for g in groups:
                     rows = slice(ROWS * g, ROWS * (g + 1))
                     nc.tensor.matmul_mx(
                         out=z[g][:, c * CHUNK + n0 : c * CHUNK + n0 + MM_N],
@@ -109,11 +113,11 @@ def tile_rows_rnx_prod_kernel(tc, x, w, xb, hs, wo, bo, out):
             )
             nc.sync.dma_start(out=h_k[c][ROWS * g : ROWS * (g + 1), :, :], in_=h_e[c][:, g, :])
 
-        def second_product(c):
+        def second_product(c, lo, hi, acc):
             for h in range(O // P):
-                for n0 in range(0, CHUNK, MM_N):
+                for n0 in range(lo, hi, MM_N):
                     nc.tensor.matmul_mx(
-                        out=u[c][h][:, n0 : n0 + MM_N],
+                        out=acc[h][:, n0 - lo : n0 - lo + MM_N],
                         lhsT=wo_op[1][:, h * P : (h + 1) * P].bitcast(FP8X4),
                         lhsT_scale=wo_op[2][:, h * P : (h + 1) * P],
                         rhs=h_op[c][1][:, n0 : n0 + MM_N].bitcast(FP8X4),
@@ -121,29 +125,49 @@ def tile_rows_rnx_prod_kernel(tc, x, w, xb, hs, wo, bo, out):
                         start=True,
                         stop=True,
                     )
+
+        def finish(c, lo, hi, acc):
             for h in range(O // P):
-                nc.scalar.activation(out=y[c][:, h, :], in_=u[c][h][:], func=ACT.Tanh, bias=vec[:, 16 * h + 1 : 16 * h + 2])
-            nc.sync.dma_start(out=out_p[:, :, cols(c)], in_=y[c][:])
+                nc.scalar.activation(
+                    out=y[c][:, h, lo:hi], in_=acc[h], func=ACT.Tanh, bias=vec[:, 16 * h + 1 : 16 * h + 2]
+                )
+            nc.sync.dma_start(out=out_p[:, :, c * CHUNK + lo : c * CHUNK + hi], in_=y[c][:, :, lo:hi])
 
         interleave("scalar", w_op[0], w_raw, 0, E)
-        nc.vector.transpose(out=vec[:], in_=vec_rows[:])
         interleave("vector", x_op[0][0], x_raw[0], 0, 176)
         interleave("scalar", x_op[0][0], x_raw[0], 176, CHUNK)
-        quantize(w_op)
-        quantize(x_op[0])
-        first_product(0)
-        interleave("scalar", x_op[1][0], x_raw[1], 96, CHUNK)
-        for g in (0, 2, 1, 3):
+        nc.vector.transpose(out=vec[:], in_=vec_rows[:])
+        quantize(w_op, 0, E)
+        quantize(x_op[0], 0, CHUNK)
+        first_product(0, range(G))
+        interleave("vector", x_op[1][0], x_raw[1], 0, 176)
+        interleave("scalar", x_op[1][0], x_raw[1], 176, CHUNK)
+        fuse(0, 0)
+        quantize(x_op[1], 0, CHUNK)
+        first_product(1, [0])
+        for g in range(1, G):
             fuse(0, g)
-        interleave("vector", x_op[1][0], x_raw[1], 0, 96)
-        quantize(x_op[1])
-        first_product(1)
-        interleave("scalar", wo_op[0], wo_raw, 0, O)
-        for g in (0, 2, 1, 3):
+            first_product(1, [g])
+        for g in range(G):
             fuse(1, g)
-        quantize(wo_op)
-        for c in range(chunks):
-            interleave("vector", h_op[c][0], h_k[c], 0, 176)
-            interleave("scalar", h_op[c][0], h_k[c], 176, CHUNK)
-            quantize(h_op[c])
-            second_product(c)
+        interleave("scalar", wo_op[0], wo_raw, 0, P)
+        interleave("vector", wo_op[0], wo_raw, P, O)
+        quantize(wo_op, 0, O)
+
+        acc0 = [u[0][:], u[1][:]]
+        acc_a = [u[2][:, 0:MM_N], u[2][:, MM_N:CHUNK]]
+        acc_b = [u[3][:, 0:MM_N], u[3][:, MM_N:CHUNK]]
+        interleave("vector", h_op[0][0], h_k[0], 0, 176)
+        interleave("scalar", h_op[0][0], h_k[0], 176, CHUNK)
+        quantize(h_op[0], 0, CHUNK)
+        second_product(0, 0, CHUNK, acc0)
+        interleave("vector", h_op[1][0], h_k[1], 0, MM_N)
+        interleave("scalar", h_op[1][0], h_k[1], 192, CHUNK)
+        interleave("vector", h_op[1][0], h_k[1], MM_N, 192)
+        finish(0, 0, CHUNK, acc0)
+        quantize(h_op[1], 0, MM_N)
+        second_product(1, 0, MM_N, acc_a)
+        quantize(h_op[1], MM_N, CHUNK)
+        second_product(1, MM_N, CHUNK, acc_b)
+        finish(1, 0, MM_N, acc_a)
+        finish(1, MM_N, CHUNK, acc_b)

@@ -45,11 +45,12 @@ def tile_rows_rnx_prod_kernel(tc, x, w, xb, hs, wo, bo, out):
             )
 
         def interleave(engine, dst, src, lo, hi):
-            view = src[:, :, lo:hi].rearrange("p j n -> p n j")
+            view = src[:, :, lo:hi].rearrange("p j (c i) -> p c j i", i=4)
+            into = dst[:, lo:hi, :].rearrange("p (c i) j -> p c j i", i=4)
             if engine == "scalar":
-                nc.scalar.copy(out=dst[:, lo:hi, :], in_=view)
+                nc.scalar.copy(out=into, in_=view)
             else:
-                nc.vector.tensor_copy(out=dst[:, lo:hi, :], in_=view)
+                nc.vector.tensor_copy(out=into, in_=view)
 
         def quantize(op, lo, hi):
             bf, codes, scales = op
@@ -80,8 +81,8 @@ def tile_rows_rnx_prod_kernel(tc, x, w, xb, hs, wo, bo, out):
             return slice(c * CHUNK, (c + 1) * CHUNK)
 
         nc.vector.memset(vec_rows[:], 0.0)
-        nc.sync.dma_start(out=w_raw[:], in_=w_k)
         nc.sync.dma_start(out=x_raw[0][:], in_=x_k[:, :, cols(0)])
+        nc.sync.dma_start(out=w_raw[:], in_=w_k)
         nc.sync.dma_start(out=vec_rows[0:P:8, :], in_=hs.rearrange("g (q i) o -> q g (i o)", i=ROWS))
         nc.sync.dma_start(out=vec_rows[1:P:16, :], in_=bo.rearrange("(h q i) o -> q h (i o)", h=O // P, i=ROWS))
         nc.sync.dma_start(out=x_raw[1][:], in_=x_k[:, :, cols(1)])
@@ -93,8 +94,8 @@ def tile_rows_rnx_prod_kernel(tc, x, w, xb, hs, wo, bo, out):
         nc.scalar.activation(out=warm[:], in_=warm[:], func=ACT.Tanh)
 
         def first_product(c, groups):
-            for n0 in range(0, CHUNK, MM_N):
-                for g in groups:
+            for g in groups:
+                for n0 in range(0, CHUNK, MM_N):
                     rows = slice(ROWS * g, ROWS * (g + 1))
                     nc.tensor.matmul_mx(
                         out=z[g][:, c * CHUNK + n0 : c * CHUNK + n0 + MM_N],
@@ -126,19 +127,22 @@ def tile_rows_rnx_prod_kernel(tc, x, w, xb, hs, wo, bo, out):
                         stop=True,
                     )
 
-        def finish(c, lo, hi, acc):
-            for h in range(O // P):
+        def finish(c, lo, hi, acc, halves=range(O // P)):
+            for h in halves:
                 nc.scalar.activation(
                     out=y[c][:, h, lo:hi], in_=acc[h], func=ACT.Tanh, bias=vec[:, 16 * h + 1 : 16 * h + 2]
                 )
-            nc.sync.dma_start(out=out_p[:, :, c * CHUNK + lo : c * CHUNK + hi], in_=y[c][:, :, lo:hi])
 
-        interleave("scalar", w_op[0], w_raw, 0, E)
+        def store(c, lo, hi, halves=slice(0, O // P)):
+            nc.sync.dma_start(out=out_p[:, halves, c * CHUNK + lo : c * CHUNK + hi], in_=y[c][:, halves, lo:hi])
+
         interleave("vector", x_op[0][0], x_raw[0], 0, 176)
         interleave("scalar", x_op[0][0], x_raw[0], 176, CHUNK)
-        nc.vector.transpose(out=vec[:], in_=vec_rows[:])
-        quantize(w_op, 0, E)
+        interleave("vector", w_op[0], w_raw, 0, 64)
+        interleave("scalar", w_op[0], w_raw, 64, E)
         quantize(x_op[0], 0, CHUNK)
+        quantize(w_op, 0, E)
+        nc.vector.transpose(out=vec[:], in_=vec_rows[:])
         first_product(0, range(G))
         interleave("vector", x_op[1][0], x_raw[1], 0, 176)
         interleave("scalar", x_op[1][0], x_raw[1], 176, CHUNK)
@@ -150,24 +154,32 @@ def tile_rows_rnx_prod_kernel(tc, x, w, xb, hs, wo, bo, out):
             first_product(1, [g])
         for g in range(G):
             fuse(1, g)
-        interleave("scalar", wo_op[0], wo_raw, 0, P)
-        interleave("vector", wo_op[0], wo_raw, P, O)
-        quantize(wo_op, 0, O)
+        def acc(piece):
+            if piece == 3:
+                return [u[2][:, 0:MM_N], u[3][:, 0:MM_N]]
+            return [u[piece % 2][:, 0:MM_N], u[piece % 2][:, MM_N:CHUNK]]
 
-        acc0 = [u[0][:], u[1][:]]
-        acc_a = [u[2][:, 0:MM_N], u[2][:, MM_N:CHUNK]]
-        acc_b = [u[3][:, 0:MM_N], u[3][:, MM_N:CHUNK]]
-        interleave("vector", h_op[0][0], h_k[0], 0, 176)
-        interleave("scalar", h_op[0][0], h_k[0], 176, CHUNK)
-        quantize(h_op[0], 0, CHUNK)
-        second_product(0, 0, CHUNK, acc0)
+        interleave("vector", wo_op[0], wo_raw, 0, 176)
+        interleave("scalar", wo_op[0], wo_raw, 176, O)
+        interleave("vector", h_op[0][0], h_k[0], 0, MM_N)
+        interleave("scalar", h_op[0][0], h_k[0], MM_N, CHUNK)
+        quantize(wo_op, 0, O)
+        quantize(h_op[0], 0, MM_N)
+        second_product(0, 0, MM_N, acc(0))
+        quantize(h_op[0], MM_N, CHUNK)
+        second_product(0, MM_N, CHUNK, acc(1))
         interleave("vector", h_op[1][0], h_k[1], 0, MM_N)
         interleave("scalar", h_op[1][0], h_k[1], 192, CHUNK)
         interleave("vector", h_op[1][0], h_k[1], MM_N, 192)
-        finish(0, 0, CHUNK, acc0)
+        finish(0, 0, MM_N, acc(0))
+        finish(0, MM_N, CHUNK, acc(1))
+        store(0, 0, CHUNK)
         quantize(h_op[1], 0, MM_N)
-        second_product(1, 0, MM_N, acc_a)
+        second_product(1, 0, MM_N, acc(2))
         quantize(h_op[1], MM_N, CHUNK)
-        second_product(1, MM_N, CHUNK, acc_b)
-        finish(1, 0, MM_N, acc_a)
-        finish(1, MM_N, CHUNK, acc_b)
+        second_product(1, MM_N, CHUNK, acc(3))
+        finish(1, 0, MM_N, acc(2))
+        store(1, 0, MM_N)
+        for h in range(O // P):
+            finish(1, MM_N, CHUNK, acc(3), [h])
+            store(1, MM_N, CHUNK, slice(h, h + 1))

@@ -64,12 +64,12 @@ def tile_rows_rnx_prod_kernel(tc, x, w, xb, hs, wo, bo, out):
         wo_raw = tile("wo_raw", [P, PACK, O], F32)
         vec_rows = tile("vec_rows", [P, ROWS], F32)
         vec = tile("vec", [P, ROWS], F32)
-        warm = tile("warm", [P, 1], F32)
         x_raw = [tile("x_raw%d" % c, [P, PACK, CHUNK], F32) for c in range(chunks)]
         xb_t = [tile("xb_t%d" % c, [P, G, CHUNK], F32) for c in range(chunks)]
         h_e = [tile("h_e%d" % c, [P, G, CHUNK], BF16) for c in range(chunks)]
         h_k = [tile("h_k%d" % c, [P, PACK, CHUNK], BF16) for c in range(chunks)]
         y = [tile("y%d" % c, [P, O // P, CHUNK], F32) for c in range(chunks)]
+        zs = [tile("zs%d" % c, [P, CHUNK], F32) for c in range(chunks)]
         w_op = operand("w", E)
         wo_op = operand("wo", O)
         x_op = [operand("x%d" % c, CHUNK) for c in range(chunks)]
@@ -90,8 +90,6 @@ def tile_rows_rnx_prod_kernel(tc, x, w, xb, hs, wo, bo, out):
             nc.sync.dma_start(out=xb_t[c][:, 0:2, :], in_=xb_e[:, 0:2, cols(c)])
             nc.sync.dma_start(out=xb_t[c][:, 2:4, :], in_=xb_e[:, 2:4, cols(c)])
         nc.sync.dma_start(out=wo_raw[:], in_=wo_k)
-        nc.vector.memset(warm[:], 0.0)
-        nc.scalar.activation(out=warm[:], in_=warm[:], func=ACT.Tanh)
 
         def first_product(c, groups):
             for g in groups:
@@ -112,7 +110,15 @@ def tile_rows_rnx_prod_kernel(tc, x, w, xb, hs, wo, bo, out):
                 out=h_e[c][:, g, :], in0=z[g][:, cols(c)], scalar=vec[:, 8 * g : 8 * g + 1], in1=xb_t[c][:, g, :],
                 op0=ALU.mult, op1=ALU.mult,
             )
-            nc.sync.dma_start(out=h_k[c][ROWS * g : ROWS * (g + 1), :, :], in_=h_e[c][:, g, :])
+
+        def move(c, g, queue=nc.sync):
+            queue.dma_start(out=h_k[c][ROWS * g : ROWS * (g + 1), :, :], in_=h_e[c][:, g, :])
+
+        def scale_out(c, g):
+            nc.scalar.activation(out=zs[c][:], in_=z[g][:, cols(c)], func=ACT.Copy, scale=vec[:, 8 * g : 8 * g + 1])
+
+        def times_xb(c, g):
+            nc.gpsimd.tensor_tensor(out=h_e[c][:, g, :], in0=zs[c][:], in1=xb_t[c][:, g, :], op=ALU.mult)
 
         def second_product(c, lo, hi, acc):
             for h in range(O // P):
@@ -146,14 +152,26 @@ def tile_rows_rnx_prod_kernel(tc, x, w, xb, hs, wo, bo, out):
         first_product(0, range(G))
         interleave("vector", x_op[1][0], x_raw[1], 0, 176)
         interleave("scalar", x_op[1][0], x_raw[1], 176, CHUNK)
+        scale_out(0, 1)
         fuse(0, 0)
+        move(0, 0)
         quantize(x_op[1], 0, CHUNK)
-        first_product(1, [0])
-        for g in range(1, G):
+        times_xb(0, 1)
+        first_product(1, [0, 1])
+        scale_out(1, 0)
+        times_xb(1, 0)
+        for g in (2, 3):
             fuse(0, g)
+            move(0, g)
             first_product(1, [g])
-        for g in range(G):
+        move(0, 1, nc.scalar)
+        for g in (1, 2):
             fuse(1, g)
+            move(1, g)
+        move(1, 0, nc.scalar)
+        fuse(1, 3)
+        move(1, 3)
+
         def acc(piece):
             if piece == 3:
                 return [u[2][:, 0:MM_N], u[3][:, 0:MM_N]]

@@ -86,10 +86,8 @@ def tile_rows_rnx_prod_kernel(tc, x, w, xb, hs, wo, bo, out):
         nc.sync.dma_start(out=vec_rows[0:P:8, :], in_=hs.rearrange("g (q i) o -> q g (i o)", i=ROWS))
         nc.sync.dma_start(out=vec_rows[1:P:16, :], in_=bo.rearrange("(h q i) o -> q h (i o)", h=O // P, i=ROWS))
         nc.sync.dma_start(out=x_raw[1][:], in_=x_k[:, :, cols(1)])
-        for c in range(chunks):
-            nc.sync.dma_start(out=xb_t[c][:, 0:2, :], in_=xb_e[:, 0:2, cols(c)])
-            nc.sync.dma_start(out=xb_t[c][:, 2:4, :], in_=xb_e[:, 2:4, cols(c)])
-        nc.sync.dma_start(out=wo_raw[:], in_=wo_k)
+        for c, lo, hi in ((0, 0, 2), (0, 2, 4), (1, 0, 2), (1, 2, 3), (1, 3, 4)):
+            nc.sync.dma_start(out=xb_t[c][:, lo:hi, :], in_=xb_e[:, lo:hi, cols(c)])
 
         def first_product(c, groups):
             for g in groups:
@@ -153,22 +151,24 @@ def tile_rows_rnx_prod_kernel(tc, x, w, xb, hs, wo, bo, out):
         interleave("vector", x_op[1][0], x_raw[1], 0, 176)
         interleave("scalar", x_op[1][0], x_raw[1], 176, CHUNK)
         scale_out(0, 1)
-        fuse(0, 0)
-        move(0, 0)
         quantize(x_op[1], 0, CHUNK)
         times_xb(0, 1)
-        first_product(1, [0, 1])
-        scale_out(1, 0)
-        times_xb(1, 0)
+        first_product(1, [1])
+        scale_out(1, 1)
+        times_xb(1, 1)
+        fuse(0, 0)
+        move(0, 0, nc.scalar)
+        nc.sync.dma_start(out=wo_raw[:], in_=wo_k)
+        first_product(1, [0])
         for g in (2, 3):
             fuse(0, g)
             move(0, g)
             first_product(1, [g])
         move(0, 1, nc.scalar)
-        for g in (1, 2):
+        for g in (0, 2):
             fuse(1, g)
             move(1, g)
-        move(1, 0, nc.scalar)
+        move(1, 1, nc.scalar)
         fuse(1, 3)
         move(1, 3)
 

@@ -52,6 +52,14 @@ def tile_rows_rnx_prod_kernel(tc, x, w, xb, hs, wo, bo, out):
             else:
                 nc.vector.tensor_copy(out=into, in_=view)
 
+        def interleave_pair(engine, a, c, lo, hi):
+            view = x_raw[a][:, :, c * CHUNK + lo : c * CHUNK + hi].rearrange("p j (c i) -> p c j i", i=4)
+            into = x_op[c][0][:, lo:hi, 2 * a : 2 * a + 2].rearrange("p (c i) j -> p c j i", i=4)
+            if engine == "scalar":
+                nc.scalar.copy(out=into, in_=view)
+            else:
+                nc.vector.tensor_copy(out=into, in_=view)
+
         def quantize(op, lo, hi):
             bf, codes, scales = op
             nc.vector.quantize_mx(
@@ -64,8 +72,9 @@ def tile_rows_rnx_prod_kernel(tc, x, w, xb, hs, wo, bo, out):
         wo_raw = tile("wo_raw", [P, PACK, O], F32)
         vec_rows = tile("vec_rows", [P, ROWS], F32)
         vec = tile("vec", [P, ROWS], F32)
-        x_raw = [tile("x_raw%d" % c, [P, PACK, CHUNK], F32) for c in range(chunks)]
-        xb_t = [tile("xb_t%d" % c, [P, G, CHUNK], F32) for c in range(chunks)]
+        x_raw = [tile("x_raw%d" % a, [P, 2, N], F32) for a in range(2)]
+        xb_w = [tile("xb_w%d" % g, [P, N], F32) for g in range(2)]
+        xb_t = [tile("xb_t%d" % c, [P, 2, CHUNK], F32) for c in range(chunks)]
         h_e = [tile("h_e%d" % c, [P, G, CHUNK], BF16) for c in range(chunks)]
         h_k = [tile("h_k%d" % c, [P, PACK, CHUNK], BF16) for c in range(chunks)]
         y = [tile("y%d" % c, [P, O // P, CHUNK], F32) for c in range(chunks)]
@@ -81,13 +90,18 @@ def tile_rows_rnx_prod_kernel(tc, x, w, xb, hs, wo, bo, out):
             return slice(c * CHUNK, (c + 1) * CHUNK)
 
         nc.vector.memset(vec_rows[:], 0.0)
-        nc.sync.dma_start(out=x_raw[0][:], in_=x_k[:, :, cols(0)])
+        nc.sync.dma_start(out=x_raw[0][:], in_=x_k[:, 0:2, :])
         nc.sync.dma_start(out=w_raw[:], in_=w_k)
         nc.sync.dma_start(out=vec_rows[0:P:8, :], in_=hs.rearrange("g (q i) o -> q g (i o)", i=ROWS))
         nc.sync.dma_start(out=vec_rows[1:P:16, :], in_=bo.rearrange("(h q i) o -> q h (i o)", h=O // P, i=ROWS))
-        nc.sync.dma_start(out=x_raw[1][:], in_=x_k[:, :, cols(1)])
-        for c, lo, hi in ((0, 0, 2), (0, 2, 4), (1, 0, 2), (1, 2, 3), (1, 3, 4)):
-            nc.sync.dma_start(out=xb_t[c][:, lo:hi, :], in_=xb_e[:, lo:hi, cols(c)])
+        nc.sync.dma_start(out=x_raw[1][:], in_=x_k[:, 2:4, :])
+        for g in (1, 0):
+            nc.sync.dma_start(out=xb_w[g][:], in_=xb_e[:, g, :])
+        for c, lo, hi in ((0, 2, 4), (1, 2, 3), (1, 3, 4)):
+            nc.sync.dma_start(out=xb_t[c][:, lo - 2 : hi - 2, :], in_=xb_e[:, lo:hi, cols(c)])
+
+        def xb_of(c, g):
+            return xb_w[g][:, cols(c)] if g < 2 else xb_t[c][:, g - 2, :]
 
         def first_product(c, groups):
             for g in groups:
@@ -105,7 +119,7 @@ def tile_rows_rnx_prod_kernel(tc, x, w, xb, hs, wo, bo, out):
 
         def fuse(c, g):
             nc.vector.scalar_tensor_tensor(
-                out=h_e[c][:, g, :], in0=z[g][:, cols(c)], scalar=vec[:, 8 * g : 8 * g + 1], in1=xb_t[c][:, g, :],
+                out=h_e[c][:, g, :], in0=z[g][:, cols(c)], scalar=vec[:, 8 * g : 8 * g + 1], in1=xb_of(c, g),
                 op0=ALU.mult, op1=ALU.mult,
             )
 
@@ -116,7 +130,7 @@ def tile_rows_rnx_prod_kernel(tc, x, w, xb, hs, wo, bo, out):
             nc.scalar.activation(out=zs[c][:], in_=z[g][:, cols(c)], func=ACT.Copy, scale=vec[:, 8 * g : 8 * g + 1])
 
         def times_xb(c, g):
-            nc.gpsimd.tensor_tensor(out=h_e[c][:, g, :], in0=zs[c][:], in1=xb_t[c][:, g, :], op=ALU.mult)
+            nc.gpsimd.tensor_tensor(out=h_e[c][:, g, :], in0=zs[c][:], in1=xb_of(c, g), op=ALU.mult)
 
         def second_product(c, lo, hi, acc):
             for h in range(O // P):
@@ -140,31 +154,34 @@ def tile_rows_rnx_prod_kernel(tc, x, w, xb, hs, wo, bo, out):
         def store(c, lo, hi, halves=slice(0, O // P)):
             nc.sync.dma_start(out=out_p[:, halves, c * CHUNK + lo : c * CHUNK + hi], in_=y[c][:, halves, lo:hi])
 
-        interleave("vector", x_op[0][0], x_raw[0], 0, 176)
-        interleave("scalar", x_op[0][0], x_raw[0], 176, CHUNK)
-        interleave("vector", w_op[0], w_raw, 0, 64)
-        interleave("scalar", w_op[0], w_raw, 64, E)
-        quantize(x_op[0], 0, CHUNK)
-        quantize(w_op, 0, E)
+        interleave_pair("vector", 0, 0, 0, CHUNK)
+        interleave_pair("scalar", 0, 1, 0, CHUNK)
+        interleave("vector", w_op[0], w_raw, 0, E)
         nc.vector.transpose(out=vec[:], in_=vec_rows[:])
-        first_product(0, range(G))
-        interleave("vector", x_op[1][0], x_raw[1], 0, 176)
-        interleave("scalar", x_op[1][0], x_raw[1], 176, CHUNK)
-        scale_out(0, 1)
+        quantize(w_op, 0, E)
+        interleave_pair("vector", 1, 0, 0, 176)
+        interleave_pair("scalar", 1, 0, 176, CHUNK)
+        interleave_pair("vector", 1, 1, 0, 128)
+        interleave_pair("scalar", 1, 1, 128, CHUNK)
+        quantize(x_op[0], 0, CHUNK)
+        first_product(0, [1, 0, 2, 3])
         quantize(x_op[1], 0, CHUNK)
+        scale_out(0, 1)
         times_xb(0, 1)
         first_product(1, [1])
-        scale_out(1, 1)
-        times_xb(1, 1)
         fuse(0, 0)
         move(0, 0, nc.scalar)
         nc.sync.dma_start(out=wo_raw[:], in_=wo_k)
+        scale_out(1, 1)
+        times_xb(1, 1)
         first_product(1, [0])
-        for g in (2, 3):
-            fuse(0, g)
-            move(0, g)
-            first_product(1, [g])
-        move(0, 1, nc.scalar)
+        fuse(0, 2)
+        move(0, 2)
+        move(0, 1)
+        first_product(1, [2])
+        fuse(0, 3)
+        move(0, 3)
+        first_product(1, [3])
         for g in (0, 2):
             fuse(1, g)
             move(1, g)

@@ -73,8 +73,8 @@ def tile_rows_rnx_prod_kernel(tc, x, w, xb, hs, wo, bo, out):
         vec_rows = tile("vec_rows", [P, ROWS], F32)
         vec = tile("vec", [P, ROWS], F32)
         x_raw = [tile("x_raw%d" % a, [P, 2, N], F32) for a in range(2)]
-        xb_w = [tile("xb_w%d" % g, [P, N], F32) for g in range(2)]
-        xb_t = [tile("xb_t%d" % c, [P, 2, CHUNK], F32) for c in range(chunks)]
+        xb_w = tile("xb_w", [P, N], F32)
+        xb_t = [tile("xb_t%d" % c, [P, 3, CHUNK], F32) for c in range(chunks)]
         h_e = [tile("h_e%d" % c, [P, G, CHUNK], BF16) for c in range(chunks)]
         h_k = [tile("h_k%d" % c, [P, PACK, CHUNK], BF16) for c in range(chunks)]
         y = [tile("y%d" % c, [P, O // P, CHUNK], F32) for c in range(chunks)]
@@ -84,7 +84,11 @@ def tile_rows_rnx_prod_kernel(tc, x, w, xb, hs, wo, bo, out):
         x_op = [operand("x%d" % c, CHUNK) for c in range(chunks)]
         h_op = [operand("h%d" % c, CHUNK) for c in range(chunks)]
         z = [ps.tile([P, N], F32, name="z%d" % g) for g in range(G)]
-        u = [ps.tile([P, CHUNK], F32, name="u%d" % i) for i in range(4)]
+        z_late = ps.tile([P, CHUNK], F32, name="z_late")
+        u = [ps.tile([P, CHUNK], F32, name="u%d" % i) for i in range(3)]
+
+        def z_of(c, g):
+            return z_late[:] if (c, g) == (1, 1) else z[g][:, c * CHUNK : (c + 1) * CHUNK]
 
         def cols(c):
             return slice(c * CHUNK, (c + 1) * CHUNK)
@@ -95,20 +99,20 @@ def tile_rows_rnx_prod_kernel(tc, x, w, xb, hs, wo, bo, out):
         nc.sync.dma_start(out=vec_rows[0:P:8, :], in_=hs.rearrange("g (q i) o -> q g (i o)", i=ROWS))
         nc.sync.dma_start(out=vec_rows[1:P:16, :], in_=bo.rearrange("(h q i) o -> q h (i o)", h=O // P, i=ROWS))
         nc.sync.dma_start(out=x_raw[1][:], in_=x_k[:, 2:4, :])
-        for g in (1, 0):
-            nc.sync.dma_start(out=xb_w[g][:], in_=xb_e[:, g, :])
-        for c, lo, hi in ((0, 2, 4), (1, 2, 3), (1, 3, 4)):
-            nc.sync.dma_start(out=xb_t[c][:, lo - 2 : hi - 2, :], in_=xb_e[:, lo:hi, cols(c)])
+        nc.sync.dma_start(out=xb_w[:], in_=xb_e[:, 0, :])
+        for c in range(chunks):
+            nc.sync.dma_start(out=xb_t[c][:, 0:2, :], in_=xb_e[:, 1:3, cols(c)])
+            nc.sync.dma_start(out=xb_t[c][:, 2, :], in_=xb_e[:, 3, cols(c)])
 
         def xb_of(c, g):
-            return xb_w[g][:, cols(c)] if g < 2 else xb_t[c][:, g - 2, :]
+            return xb_w[:, cols(c)] if g == 0 else xb_t[c][:, g - 1, :]
 
-        def first_product(c, groups):
+        def first_product(c, groups, starts=(0, MM_N)):
             for g in groups:
-                for n0 in range(0, CHUNK, MM_N):
+                for n0 in starts:
                     rows = slice(ROWS * g, ROWS * (g + 1))
                     nc.tensor.matmul_mx(
-                        out=z[g][:, c * CHUNK + n0 : c * CHUNK + n0 + MM_N],
+                        out=z_of(c, g)[:, n0 : n0 + MM_N],
                         lhsT=w_op[1][rows, :].bitcast(FP8X4),
                         lhsT_scale=w_op[2][rows, :],
                         rhs=x_op[c][1][rows, n0 : n0 + MM_N].bitcast(FP8X4),
@@ -119,7 +123,7 @@ def tile_rows_rnx_prod_kernel(tc, x, w, xb, hs, wo, bo, out):
 
         def fuse(c, g):
             nc.vector.scalar_tensor_tensor(
-                out=h_e[c][:, g, :], in0=z[g][:, cols(c)], scalar=vec[:, 8 * g : 8 * g + 1], in1=xb_of(c, g),
+                out=h_e[c][:, g, :], in0=z_of(c, g), scalar=vec[:, 8 * g : 8 * g + 1], in1=xb_of(c, g),
                 op0=ALU.mult, op1=ALU.mult,
             )
 
@@ -127,7 +131,7 @@ def tile_rows_rnx_prod_kernel(tc, x, w, xb, hs, wo, bo, out):
             queue.dma_start(out=h_k[c][ROWS * g : ROWS * (g + 1), :, :], in_=h_e[c][:, g, :])
 
         def scale_out(c, g):
-            nc.scalar.activation(out=zs[c][:], in_=z[g][:, cols(c)], func=ACT.Copy, scale=vec[:, 8 * g : 8 * g + 1])
+            nc.scalar.activation(out=zs[c][:], in_=z_of(c, g), func=ACT.Copy, scale=vec[:, 8 * g : 8 * g + 1])
 
         def times_xb(c, g):
             nc.gpsimd.tensor_tensor(out=h_e[c][:, g, :], in0=zs[c][:], in1=xb_of(c, g), op=ALU.mult)
@@ -159,16 +163,19 @@ def tile_rows_rnx_prod_kernel(tc, x, w, xb, hs, wo, bo, out):
         interleave("vector", w_op[0], w_raw, 0, E)
         nc.vector.transpose(out=vec[:], in_=vec_rows[:])
         quantize(w_op, 0, E)
-        interleave_pair("vector", 1, 0, 0, 176)
-        interleave_pair("scalar", 1, 0, 176, CHUNK)
-        interleave_pair("vector", 1, 1, 0, 128)
-        interleave_pair("scalar", 1, 1, 128, CHUNK)
-        quantize(x_op[0], 0, CHUNK)
-        first_product(0, [1, 0, 2, 3])
+        interleave_pair("vector", 1, 0, 0, MM_N)
+        interleave_pair("scalar", 1, 0, MM_N, CHUNK)
+        interleave_pair("vector", 1, 1, 0, MM_N)
+        interleave_pair("scalar", 1, 1, MM_N, CHUNK)
+        quantize(x_op[0], 0, MM_N)
+        first_product(0, [1, 0], [0])
+        quantize(x_op[0], MM_N, CHUNK)
+        first_product(0, [1, 0], [MM_N])
+        first_product(0, [2, 3])
         quantize(x_op[1], 0, CHUNK)
+        first_product(1, [1])
         scale_out(0, 1)
         times_xb(0, 1)
-        first_product(1, [1])
         fuse(0, 0)
         move(0, 0, nc.scalar)
         nc.sync.dma_start(out=wo_raw[:], in_=wo_k)
@@ -177,10 +184,10 @@ def tile_rows_rnx_prod_kernel(tc, x, w, xb, hs, wo, bo, out):
         first_product(1, [0])
         fuse(0, 2)
         move(0, 2)
-        move(0, 1)
         first_product(1, [2])
         fuse(0, 3)
         move(0, 3)
+        move(0, 1)
         first_product(1, [3])
         for g in (0, 2):
             fuse(1, g)
@@ -191,7 +198,7 @@ def tile_rows_rnx_prod_kernel(tc, x, w, xb, hs, wo, bo, out):
 
         def acc(piece):
             if piece == 3:
-                return [u[2][:, 0:MM_N], u[3][:, 0:MM_N]]
+                return [u[2][:, 0:MM_N], u[1][:, 0:MM_N]]
             return [u[piece % 2][:, 0:MM_N], u[piece % 2][:, MM_N:CHUNK]]
 
         interleave("vector", wo_op[0], wo_raw, 0, 176)

@@ -84,11 +84,10 @@ def tile_rows_rnx_prod_kernel(tc, x, w, xb, hs, wo, bo, out):
         x_op = [operand("x%d" % c, CHUNK) for c in range(chunks)]
         h_op = [operand("h%d" % c, CHUNK) for c in range(chunks)]
         z = [ps.tile([P, N], F32, name="z%d" % g) for g in range(G)]
-        z_late = ps.tile([P, CHUNK], F32, name="z_late")
-        u = [ps.tile([P, CHUNK], F32, name="u%d" % i) for i in range(3)]
+        u = [ps.tile([P, CHUNK], F32, name="u%d" % i) for i in range(4)]
 
         def z_of(c, g):
-            return z_late[:] if (c, g) == (1, 1) else z[g][:, c * CHUNK : (c + 1) * CHUNK]
+            return z[g][:, c * CHUNK : (c + 1) * CHUNK]
 
         def cols(c):
             return slice(c * CHUNK, (c + 1) * CHUNK)
@@ -136,26 +135,22 @@ def tile_rows_rnx_prod_kernel(tc, x, w, xb, hs, wo, bo, out):
         def times_xb(c, g):
             nc.gpsimd.tensor_tensor(out=h_e[c][:, g, :], in0=zs[c][:], in1=xb_of(c, g), op=ALU.mult)
 
-        def second_product(c, lo, hi, acc):
+        def second_product(c, n0, acc):
             for h in range(O // P):
-                for n0 in range(lo, hi, MM_N):
-                    nc.tensor.matmul_mx(
-                        out=acc[h][:, n0 - lo : n0 - lo + MM_N],
-                        lhsT=wo_op[1][:, h * P : (h + 1) * P].bitcast(FP8X4),
-                        lhsT_scale=wo_op[2][:, h * P : (h + 1) * P],
-                        rhs=h_op[c][1][:, n0 : n0 + MM_N].bitcast(FP8X4),
-                        rhs_scale=h_op[c][2][:, n0 : n0 + MM_N],
-                        start=True,
-                        stop=True,
-                    )
-
-        def finish(c, lo, hi, acc, halves=range(O // P)):
-            for h in halves:
-                nc.scalar.activation(
-                    out=y[c][:, h, lo:hi], in_=acc[h], func=ACT.Tanh, bias=vec[:, 16 * h + 1 : 16 * h + 2]
+                nc.tensor.matmul_mx(
+                    out=acc[h],
+                    lhsT=wo_op[1][:, h * P : (h + 1) * P].bitcast(FP8X4),
+                    lhsT_scale=wo_op[2][:, h * P : (h + 1) * P],
+                    rhs=h_op[c][1][:, n0 : n0 + MM_N].bitcast(FP8X4),
+                    rhs_scale=h_op[c][2][:, n0 : n0 + MM_N],
+                    start=True,
+                    stop=True,
                 )
 
-        def store(c, lo, hi, halves=slice(0, O // P)):
+        def finish(c, h, lo, hi, acc):
+            nc.scalar.activation(out=y[c][:, h, lo:hi], in_=acc, func=ACT.Tanh, bias=vec[:, 16 * h + 1 : 16 * h + 2])
+
+        def store(c, halves, lo, hi):
             nc.sync.dma_start(out=out_p[:, halves, c * CHUNK + lo : c * CHUNK + hi], in_=y[c][:, halves, lo:hi])
 
         interleave_pair("vector", 0, 0, 0, CHUNK)
@@ -173,9 +168,9 @@ def tile_rows_rnx_prod_kernel(tc, x, w, xb, hs, wo, bo, out):
         first_product(0, [1, 0], [MM_N])
         first_product(0, [2, 3])
         quantize(x_op[1], 0, CHUNK)
-        first_product(1, [1])
         scale_out(0, 1)
         times_xb(0, 1)
+        first_product(1, [1])
         fuse(0, 0)
         move(0, 0, nc.scalar)
         nc.sync.dma_start(out=wo_raw[:], in_=wo_k)
@@ -196,32 +191,29 @@ def tile_rows_rnx_prod_kernel(tc, x, w, xb, hs, wo, bo, out):
         fuse(1, 3)
         move(1, 3)
 
-        def acc(piece):
-            if piece == 3:
-                return [u[2][:, 0:MM_N], u[1][:, 0:MM_N]]
-            return [u[piece % 2][:, 0:MM_N], u[piece % 2][:, MM_N:CHUNK]]
-
         interleave("vector", wo_op[0], wo_raw, 0, 176)
         interleave("scalar", wo_op[0], wo_raw, 176, O)
         interleave("vector", h_op[0][0], h_k[0], 0, MM_N)
         interleave("scalar", h_op[0][0], h_k[0], MM_N, CHUNK)
         quantize(wo_op, 0, O)
-        quantize(h_op[0], 0, MM_N)
-        second_product(0, 0, MM_N, acc(0))
-        quantize(h_op[0], MM_N, CHUNK)
-        second_product(0, MM_N, CHUNK, acc(1))
+        for n0 in (0, MM_N):
+            quantize(h_op[0], n0, n0 + MM_N)
+            second_product(0, n0, [u[h][:, n0 : n0 + MM_N] for h in range(2)])
         interleave("vector", h_op[1][0], h_k[1], 0, MM_N)
         interleave("scalar", h_op[1][0], h_k[1], 192, CHUNK)
         interleave("vector", h_op[1][0], h_k[1], MM_N, 192)
-        finish(0, 0, MM_N, acc(0))
-        finish(0, MM_N, CHUNK, acc(1))
-        store(0, 0, CHUNK)
+        for h in range(2):
+            finish(0, h, 0, CHUNK, u[h][:])
+            store(0, h, 0, CHUNK)
+        third = [u[2 + h][:, 0:MM_N] for h in range(2)]
+        fourth = [u[h][:, 0:MM_N] for h in range(2)]
         quantize(h_op[1], 0, MM_N)
-        second_product(1, 0, MM_N, acc(2))
+        second_product(1, 0, third)
         quantize(h_op[1], MM_N, CHUNK)
-        second_product(1, MM_N, CHUNK, acc(3))
-        finish(1, 0, MM_N, acc(2))
-        store(1, 0, MM_N)
-        for h in range(O // P):
-            finish(1, MM_N, CHUNK, acc(3), [h])
-            store(1, MM_N, CHUNK, slice(h, h + 1))
+        second_product(1, MM_N, fourth)
+        for h in range(2):
+            finish(1, h, 0, MM_N, third[h])
+        store(1, slice(0, 2), 0, MM_N)
+        for h in range(2):
+            finish(1, h, MM_N, CHUNK, fourth[h])
+            store(1, h, MM_N, CHUNK)

@@ -17,17 +17,22 @@ P = 128
 PACK = 4
 ROWS = 32
 MM_N = 128
-CHUNK = 256
+HALF = N // 2
+OUT_TILES = O // P
+
+POOL_GROUP = 1
+VECTOR_GROUPS = (2, 3, 0)
+WO_ON_VECTOR = 176
+H_LAST_ON_VECTOR = 192
 
 
 def tile_rows_rnx_prod_kernel(tc, x, w, xb, hs, wo, bo, out):
     nc = tc.nc
-    chunks = N // CHUNK
     x_k = x.rearrange("g (p j) n -> (g p) j n", j=PACK)
     w_k = w.rearrange("g (p j) e -> (g p) j e", j=PACK)
     wo_k = wo.rearrange("g (p j) o -> (g p) j o", j=PACK)
     xb_e = xb.rearrange("g e n -> e g n")
-    out_p = out.rearrange("(h p) n -> p h n", p=P)
+    out_p = out.rearrange("(t p) n -> p t n", p=P)
 
     with ExitStack() as ctx:
         sb = ctx.enter_context(tc.tile_pool(name="sb", bufs=1))
@@ -44,21 +49,44 @@ def tile_rows_rnx_prod_kernel(tc, x, w, xb, hs, wo, bo, out):
                 tile(name + "_scales", [P, width], U8),
             )
 
-        def interleave(engine, dst, src, lo, hi):
-            view = src[:, :, lo:hi].rearrange("p j (c i) -> p c j i", i=4)
-            into = dst[:, lo:hi, :].rearrange("p (c i) j -> p c j i", i=4)
-            if engine == "scalar":
-                nc.scalar.copy(out=into, in_=view)
-            else:
-                nc.vector.tensor_copy(out=into, in_=view)
+        w_raw = tile("w_raw", [P, PACK, E], F32)
+        wo_raw = tile("wo_raw", [P, PACK, O], F32)
+        vec_rows = tile("vec_rows", [P, ROWS], F32)
+        vec = tile("vec", [P, ROWS], F32)
+        x_pair = [tile("x_pair%d" % a, [P, 2, N], F32) for a in range(2)]
+        xb_whole = [tile("xb_whole%d" % g, [P, N], F32) for g in range(2)]
+        xb_half = [tile("xb_half%d" % c, [P, 2, HALF], F32) for c in range(2)]
+        h_e = [tile("h_e%d" % c, [P, G, HALF], BF16) for c in range(2)]
+        h_k = [tile("h_k%d" % c, [P, PACK, HALF], BF16) for c in range(2)]
+        y = [tile("y%d" % c, [P, OUT_TILES, HALF], F32) for c in range(2)]
+        z_scaled = [tile("z_scaled%d" % c, [P, HALF], F32) for c in range(2)]
+        w_op = operand("w", E)
+        wo_op = operand("wo", O)
+        x_op = [operand("x%d" % c, HALF) for c in range(2)]
+        h_op = [operand("h%d" % c, HALF) for c in range(2)]
+        z = [ps.tile([P, N], F32, name="z%d" % g) for g in range(G)]
+        u = [ps.tile([P, HALF], F32, name="u%d" % i) for i in range(2 * OUT_TILES)]
 
-        def interleave_pair(engine, a, c, lo, hi):
-            view = x_raw[a][:, :, c * CHUNK + lo : c * CHUNK + hi].rearrange("p j (c i) -> p c j i", i=4)
-            into = x_op[c][0][:, lo:hi, 2 * a : 2 * a + 2].rearrange("p (c i) j -> p c j i", i=4)
-            if engine == "scalar":
-                nc.scalar.copy(out=into, in_=view)
-            else:
-                nc.vector.tensor_copy(out=into, in_=view)
+        def cols(c):
+            return slice(c * HALF, (c + 1) * HALF)
+
+        def xb_of(c, g):
+            return xb_whole[g][:, cols(c)] if g < 2 else xb_half[c][:, g - 2, :]
+
+        def hs_of(g):
+            return vec[:, 8 * g : 8 * g + 1]
+
+        def bo_of(t):
+            return vec[:, 16 * t + 1 : 16 * t + 2]
+
+        def interleave(copy, into, rows):
+            copy(out=into.rearrange("p (c i) j -> p c j i", i=4), in_=rows.rearrange("p j (c i) -> p c j i", i=4))
+
+        def interleave_op(copy, op, raw, lo, hi):
+            interleave(copy, op[0][:, lo:hi, :], raw[:, :, lo:hi])
+
+        def interleave_x(copy, a, c, lo, hi):
+            interleave(copy, x_op[c][0][:, lo:hi, 2 * a : 2 * a + 2], x_pair[a][:, :, c * HALF + lo : c * HALF + hi])
 
         def quantize(op, lo, hi):
             bf, codes, scales = op
@@ -68,152 +96,122 @@ def tile_rows_rnx_prod_kernel(tc, x, w, xb, hs, wo, bo, out):
                 in_=bf[:, lo:hi, :].rearrange("p n j -> p (n j)"),
             )
 
-        w_raw = tile("w_raw", [P, PACK, E], F32)
-        wo_raw = tile("wo_raw", [P, PACK, O], F32)
-        vec_rows = tile("vec_rows", [P, ROWS], F32)
-        vec = tile("vec", [P, ROWS], F32)
-        x_raw = [tile("x_raw%d" % a, [P, 2, N], F32) for a in range(2)]
-        xb_w = tile("xb_w", [P, N], F32)
-        xb_t = [tile("xb_t%d" % c, [P, 3, CHUNK], F32) for c in range(chunks)]
-        h_e = [tile("h_e%d" % c, [P, G, CHUNK], BF16) for c in range(chunks)]
-        h_k = [tile("h_k%d" % c, [P, PACK, CHUNK], BF16) for c in range(chunks)]
-        y = [tile("y%d" % c, [P, O // P, CHUNK], F32) for c in range(chunks)]
-        zs = [tile("zs%d" % c, [P, CHUNK], F32) for c in range(chunks)]
-        w_op = operand("w", E)
-        wo_op = operand("wo", O)
-        x_op = [operand("x%d" % c, CHUNK) for c in range(chunks)]
-        h_op = [operand("h%d" % c, CHUNK) for c in range(chunks)]
-        z = [ps.tile([P, N], F32, name="z%d" % g) for g in range(G)]
-        u = [ps.tile([P, CHUNK], F32, name="u%d" % i) for i in range(4)]
-
-        def z_of(c, g):
-            return z[g][:, c * CHUNK : (c + 1) * CHUNK]
-
-        def cols(c):
-            return slice(c * CHUNK, (c + 1) * CHUNK)
-
-        nc.vector.memset(vec_rows[:], 0.0)
-        nc.sync.dma_start(out=x_raw[0][:], in_=x_k[:, 0:2, :])
-        nc.sync.dma_start(out=w_raw[:], in_=w_k)
-        nc.sync.dma_start(out=vec_rows[0:P:8, :], in_=hs.rearrange("g (q i) o -> q g (i o)", i=ROWS))
-        nc.sync.dma_start(out=vec_rows[1:P:16, :], in_=bo.rearrange("(h q i) o -> q h (i o)", h=O // P, i=ROWS))
-        nc.sync.dma_start(out=x_raw[1][:], in_=x_k[:, 2:4, :])
-        nc.sync.dma_start(out=xb_w[:], in_=xb_e[:, 0, :])
-        for c in range(chunks):
-            nc.sync.dma_start(out=xb_t[c][:, 0:2, :], in_=xb_e[:, 1:3, cols(c)])
-            nc.sync.dma_start(out=xb_t[c][:, 2, :], in_=xb_e[:, 3, cols(c)])
-
-        def xb_of(c, g):
-            return xb_w[:, cols(c)] if g == 0 else xb_t[c][:, g - 1, :]
+        def mx_product(acc, parts, stationary, m0, moving, n0):
+            nc.tensor.matmul_mx(
+                out=acc,
+                lhsT=stationary[1][parts, m0 : m0 + P].bitcast(FP8X4),
+                lhsT_scale=stationary[2][parts, m0 : m0 + P],
+                rhs=moving[1][parts, n0 : n0 + MM_N].bitcast(FP8X4),
+                rhs_scale=moving[2][parts, n0 : n0 + MM_N],
+                start=True,
+                stop=True,
+            )
 
         def first_product(c, groups, starts=(0, MM_N)):
             for g in groups:
                 for n0 in starts:
-                    rows = slice(ROWS * g, ROWS * (g + 1))
-                    nc.tensor.matmul_mx(
-                        out=z_of(c, g)[:, n0 : n0 + MM_N],
-                        lhsT=w_op[1][rows, :].bitcast(FP8X4),
-                        lhsT_scale=w_op[2][rows, :],
-                        rhs=x_op[c][1][rows, n0 : n0 + MM_N].bitcast(FP8X4),
-                        rhs_scale=x_op[c][2][rows, n0 : n0 + MM_N],
-                        start=True,
-                        stop=True,
-                    )
+                    acc = z[g][:, c * HALF + n0 : c * HALF + n0 + MM_N]
+                    mx_product(acc, slice(ROWS * g, ROWS * (g + 1)), w_op, 0, x_op[c], n0)
 
-        def fuse(c, g):
+        def second_product(c, n0, accs):
+            for t in range(OUT_TILES):
+                mx_product(accs[t], slice(0, P), wo_op, t * P, h_op[c], n0)
+
+        def fuse_on_vector(c, g):
             nc.vector.scalar_tensor_tensor(
-                out=h_e[c][:, g, :], in0=z_of(c, g), scalar=vec[:, 8 * g : 8 * g + 1], in1=xb_of(c, g),
+                out=h_e[c][:, g, :], in0=z[g][:, cols(c)], scalar=hs_of(g), in1=xb_of(c, g),
                 op0=ALU.mult, op1=ALU.mult,
             )
 
-        def move(c, g, queue=nc.sync):
+        def fuse_on_pool(c):
+            g = POOL_GROUP
+            nc.scalar.activation(out=z_scaled[c][:], in_=z[g][:, cols(c)], func=ACT.Copy, scale=hs_of(g))
+            nc.gpsimd.tensor_tensor(out=h_e[c][:, g, :], in0=z_scaled[c][:], in1=xb_of(c, g), op=ALU.mult)
+
+        def move(c, g, queue):
             queue.dma_start(out=h_k[c][ROWS * g : ROWS * (g + 1), :, :], in_=h_e[c][:, g, :])
 
-        def scale_out(c, g):
-            nc.scalar.activation(out=zs[c][:], in_=z_of(c, g), func=ACT.Copy, scale=vec[:, 8 * g : 8 * g + 1])
+        def tanh(c, t, lo, hi, acc):
+            nc.scalar.activation(out=y[c][:, t, lo:hi], in_=acc, func=ACT.Tanh, bias=bo_of(t))
 
-        def times_xb(c, g):
-            nc.gpsimd.tensor_tensor(out=h_e[c][:, g, :], in0=zs[c][:], in1=xb_of(c, g), op=ALU.mult)
+        def store(c, t, lo, hi):
+            nc.sync.dma_start(out=out_p[:, t, c * HALF + lo : c * HALF + hi], in_=y[c][:, t, lo:hi])
 
-        def second_product(c, n0, acc):
-            for h in range(O // P):
-                nc.tensor.matmul_mx(
-                    out=acc[h],
-                    lhsT=wo_op[1][:, h * P : (h + 1) * P].bitcast(FP8X4),
-                    lhsT_scale=wo_op[2][:, h * P : (h + 1) * P],
-                    rhs=h_op[c][1][:, n0 : n0 + MM_N].bitcast(FP8X4),
-                    rhs_scale=h_op[c][2][:, n0 : n0 + MM_N],
-                    start=True,
-                    stop=True,
-                )
+        on_vector, on_scalar = nc.vector.tensor_copy, nc.scalar.copy
+        first, second, third = VECTOR_GROUPS
 
-        def finish(c, h, lo, hi, acc):
-            nc.scalar.activation(out=y[c][:, h, lo:hi], in_=acc, func=ACT.Tanh, bias=vec[:, 16 * h + 1 : 16 * h + 2])
+        nc.vector.memset(vec_rows[:], 0.0)
+        nc.sync.dma_start(out=x_pair[0][:], in_=x_k[:, 0:2, :])
+        nc.sync.dma_start(out=w_raw[:], in_=w_k)
+        nc.sync.dma_start(out=vec_rows[0:P:8, :], in_=hs.rearrange("g (q i) o -> q g (i o)", i=ROWS))
+        nc.sync.dma_start(out=vec_rows[1:P:16, :], in_=bo.rearrange("(t q i) o -> q t (i o)", t=OUT_TILES, i=ROWS))
+        nc.sync.dma_start(out=x_pair[1][:], in_=x_k[:, 2:4, :])
+        nc.sync.dma_start(out=xb_whole[1][:], in_=xb_e[:, 1, :])
+        nc.sync.dma_start(out=xb_half[0][:], in_=xb_e[:, 2:4, cols(0)])
+        nc.sync.dma_start(out=xb_whole[0][:], in_=xb_e[:, 0, :])
+        for g in (2, 3):
+            nc.sync.dma_start(out=xb_half[1][:, g - 2, :], in_=xb_e[:, g, cols(1)])
 
-        def store(c, halves, lo, hi):
-            nc.sync.dma_start(out=out_p[:, halves, c * CHUNK + lo : c * CHUNK + hi], in_=y[c][:, halves, lo:hi])
-
-        interleave_pair("vector", 0, 0, 0, CHUNK)
-        interleave_pair("scalar", 0, 1, 0, CHUNK)
-        interleave("vector", w_op[0], w_raw, 0, E)
+        interleave_x(on_vector, 0, 0, 0, HALF)
+        interleave_x(on_scalar, 0, 1, 0, HALF)
+        interleave_op(on_vector, w_op, w_raw, 0, E)
         nc.vector.transpose(out=vec[:], in_=vec_rows[:])
         quantize(w_op, 0, E)
-        interleave_pair("vector", 1, 0, 0, MM_N)
-        interleave_pair("scalar", 1, 0, MM_N, CHUNK)
-        interleave_pair("vector", 1, 1, 0, MM_N)
-        interleave_pair("scalar", 1, 1, MM_N, CHUNK)
-        quantize(x_op[0], 0, MM_N)
-        first_product(0, [1, 0], [0])
-        quantize(x_op[0], MM_N, CHUNK)
-        first_product(0, [1, 0], [MM_N])
-        first_product(0, [2, 3])
-        quantize(x_op[1], 0, CHUNK)
-        scale_out(0, 1)
-        times_xb(0, 1)
-        first_product(1, [1])
-        fuse(0, 0)
-        move(0, 0, nc.scalar)
-        nc.sync.dma_start(out=wo_raw[:], in_=wo_k)
-        scale_out(1, 1)
-        times_xb(1, 1)
-        first_product(1, [0])
-        fuse(0, 2)
-        move(0, 2)
-        first_product(1, [2])
-        fuse(0, 3)
-        move(0, 3)
-        move(0, 1)
-        first_product(1, [3])
-        for g in (0, 2):
-            fuse(1, g)
-            move(1, g)
-        move(1, 1, nc.scalar)
-        fuse(1, 3)
-        move(1, 3)
 
-        interleave("vector", wo_op[0], wo_raw, 0, 176)
-        interleave("scalar", wo_op[0], wo_raw, 176, O)
-        interleave("vector", h_op[0][0], h_k[0], 0, MM_N)
-        interleave("scalar", h_op[0][0], h_k[0], MM_N, CHUNK)
+        for c in range(2):
+            interleave_x(on_vector, 1, c, 0, MM_N)
+            interleave_x(on_scalar, 1, c, MM_N, HALF)
+        for n0 in (0, MM_N):
+            quantize(x_op[0], n0, n0 + MM_N)
+            first_product(0, [POOL_GROUP, first], [n0])
+        first_product(0, [second, third])
+        quantize(x_op[1], 0, HALF)
+
+        fuse_on_pool(0)
+        first_product(1, [POOL_GROUP])
+        fuse_on_vector(0, first)
+        move(0, first, nc.scalar)
+        nc.sync.dma_start(out=wo_raw[:], in_=wo_k)
+        fuse_on_pool(1)
+        first_product(1, [first])
+        fuse_on_vector(0, second)
+        move(0, second, nc.sync)
+        first_product(1, [second])
+        fuse_on_vector(0, third)
+        move(0, third, nc.sync)
+        move(0, POOL_GROUP, nc.sync)
+        first_product(1, [third])
+        for g in (first, second):
+            fuse_on_vector(1, g)
+            move(1, g, nc.sync)
+        move(1, POOL_GROUP, nc.scalar)
+        fuse_on_vector(1, third)
+        move(1, third, nc.sync)
+
+        interleave_op(on_vector, wo_op, wo_raw, 0, WO_ON_VECTOR)
+        interleave_op(on_scalar, wo_op, wo_raw, WO_ON_VECTOR, O)
+        interleave_op(on_vector, h_op[0], h_k[0], 0, MM_N)
+        interleave_op(on_scalar, h_op[0], h_k[0], MM_N, HALF)
         quantize(wo_op, 0, O)
         for n0 in (0, MM_N):
             quantize(h_op[0], n0, n0 + MM_N)
-            second_product(0, n0, [u[h][:, n0 : n0 + MM_N] for h in range(2)])
-        interleave("vector", h_op[1][0], h_k[1], 0, MM_N)
-        interleave("scalar", h_op[1][0], h_k[1], 192, CHUNK)
-        interleave("vector", h_op[1][0], h_k[1], MM_N, 192)
-        for h in range(2):
-            finish(0, h, 0, CHUNK, u[h][:])
-            store(0, h, 0, CHUNK)
-        third = [u[2 + h][:, 0:MM_N] for h in range(2)]
-        fourth = [u[h][:, 0:MM_N] for h in range(2)]
+            second_product(0, n0, [u[t][:, n0 : n0 + MM_N] for t in range(OUT_TILES)])
+
+        interleave_op(on_vector, h_op[1], h_k[1], 0, MM_N)
+        interleave_op(on_scalar, h_op[1], h_k[1], H_LAST_ON_VECTOR, HALF)
+        interleave_op(on_vector, h_op[1], h_k[1], MM_N, H_LAST_ON_VECTOR)
+        for t in range(OUT_TILES):
+            tanh(0, t, 0, HALF, u[t][:])
+            store(0, t, 0, HALF)
+        early = [u[OUT_TILES + t][:, 0:MM_N] for t in range(OUT_TILES)]
+        late = [u[t][:, 0:MM_N] for t in range(OUT_TILES)]
         quantize(h_op[1], 0, MM_N)
-        second_product(1, 0, third)
-        quantize(h_op[1], MM_N, CHUNK)
-        second_product(1, MM_N, fourth)
-        for h in range(2):
-            finish(1, h, 0, MM_N, third[h])
-        store(1, slice(0, 2), 0, MM_N)
-        for h in range(2):
-            finish(1, h, MM_N, CHUNK, fourth[h])
-            store(1, h, MM_N, CHUNK)
+        second_product(1, 0, early)
+        quantize(h_op[1], MM_N, HALF)
+        second_product(1, MM_N, late)
+        for t in range(OUT_TILES):
+            tanh(1, t, 0, MM_N, early[t])
+        store(1, slice(0, OUT_TILES), 0, MM_N)
+        for t in range(OUT_TILES):
+            tanh(1, t, MM_N, HALF, late[t])
+            store(1, t, MM_N, HALF)

@@ -21,7 +21,7 @@ HALF = N // 2
 OUT_TILES = O // P
 
 POOL_GROUP = 1
-VECTOR_GROUPS = (2, 3, 0)
+VECTOR_GROUPS = (2, 0, 3)
 WO_ON_VECTOR = 176
 H_LAST_ON_VECTOR = 192
 
@@ -71,7 +71,7 @@ def tile_rows_rnx_prod_kernel(tc, x, w, xb, hs, wo, bo, out):
             return slice(c * HALF, (c + 1) * HALF)
 
         def xb_of(c, g):
-            return xb_whole[g][:, cols(c)] if g < 2 else xb_half[c][:, g - 2, :]
+            return xb_whole[g // 2][:, cols(c)] if g % 2 else xb_half[c][:, g // 2, :]
 
         def hs_of(g):
             return vec[:, 8 * g : 8 * g + 1]
@@ -146,11 +146,11 @@ def tile_rows_rnx_prod_kernel(tc, x, w, xb, hs, wo, bo, out):
         nc.sync.dma_start(out=vec_rows[0:P:8, :], in_=hs.rearrange("g (q i) o -> q g (i o)", i=ROWS))
         nc.sync.dma_start(out=vec_rows[1:P:16, :], in_=bo.rearrange("(t q i) o -> q t (i o)", t=OUT_TILES, i=ROWS))
         nc.sync.dma_start(out=x_pair[1][:], in_=x_k[:, 2:4, :])
-        nc.sync.dma_start(out=xb_whole[1][:], in_=xb_e[:, 1, :])
-        nc.sync.dma_start(out=xb_half[0][:], in_=xb_e[:, 2:4, cols(0)])
-        nc.sync.dma_start(out=xb_whole[0][:], in_=xb_e[:, 0, :])
-        for g in (2, 3):
-            nc.sync.dma_start(out=xb_half[1][:, g - 2, :], in_=xb_e[:, g, cols(1)])
+        nc.sync.dma_start(out=xb_whole[0][:], in_=xb_e[:, 1, :])
+        nc.sync.dma_start(out=xb_half[0][:], in_=xb_e[:, 0:3:2, cols(0)])
+        nc.sync.dma_start(out=xb_whole[1][:], in_=xb_e[:, 3, :])
+        for g in (2, 0):
+            nc.sync.dma_start(out=xb_half[1][:, g // 2, :], in_=xb_e[:, g, cols(1)])
 
         interleave_x(on_vector, 0, 0, 0, HALF)
         interleave_x(on_scalar, 0, 1, 0, HALF)

@@ -151,6 +151,7 @@ def tile_rows_rnx_prod_kernel(tc, x, w, xb, hs, wo, bo, out):
         nc.sync.dma_start(out=xb_whole[1][:], in_=xb_e[:, 3, :])
         for g in (2, 0):
             nc.sync.dma_start(out=xb_half[1][:, g // 2, :], in_=xb_e[:, g, cols(1)])
+        nc.sync.dma_start(out=wo_raw[:], in_=wo_k)
 
         interleave_x(on_vector, 0, 0, 0, HALF)
         interleave_x(on_scalar, 0, 1, 0, HALF)
@@ -170,8 +171,7 @@ def tile_rows_rnx_prod_kernel(tc, x, w, xb, hs, wo, bo, out):
         fuse_on_pool(0)
         first_product(1, [POOL_GROUP])
         fuse_on_vector(0, first)
-        move(0, first, nc.scalar)
-        nc.sync.dma_start(out=wo_raw[:], in_=wo_k)
+        move(0, first, nc.sync)
         fuse_on_pool(1)
         first_product(1, [first])
         fuse_on_vector(0, second)

@@ -22,6 +22,7 @@ OUT_TILES = O // P
 
 POOL_GROUP = 1
 VECTOR_GROUPS = (2, 0, 3)
+LAST_ON_POOL = 192
 WO_ON_VECTOR = 176
 H_LAST_ON_VECTOR = 192
 
@@ -117,16 +118,17 @@ def tile_rows_rnx_prod_kernel(tc, x, w, xb, hs, wo, bo, out):
             for t in range(OUT_TILES):
                 mx_product(accs[t], slice(0, P), wo_op, t * P, h_op[c], n0)
 
-        def fuse_on_vector(c, g):
+        def fuse_on_vector(c, g, lo=0):
             nc.vector.scalar_tensor_tensor(
-                out=h_e[c][:, g, :], in0=z[g][:, cols(c)], scalar=hs_of(g), in1=xb_of(c, g),
+                out=h_e[c][:, g, lo:], in0=z[g][:, cols(c)][:, lo:], scalar=hs_of(g), in1=xb_of(c, g)[:, lo:],
                 op0=ALU.mult, op1=ALU.mult,
             )
 
-        def fuse_on_pool(c):
+        def fuse_on_pool(c, hi=HALF):
             g = POOL_GROUP
-            nc.scalar.activation(out=z_scaled[c][:], in_=z[g][:, cols(c)], func=ACT.Copy, scale=hs_of(g))
-            nc.gpsimd.tensor_tensor(out=h_e[c][:, g, :], in0=z_scaled[c][:], in1=xb_of(c, g), op=ALU.mult)
+            scaled = z_scaled[c][:, :hi]
+            nc.scalar.activation(out=scaled, in_=z[g][:, cols(c)][:, :hi], func=ACT.Copy, scale=hs_of(g))
+            nc.gpsimd.tensor_tensor(out=h_e[c][:, g, :hi], in0=scaled, in1=xb_of(c, g)[:, :hi], op=ALU.mult)
 
         def move(c, g, queue):
             queue.dma_start(out=h_k[c][ROWS * g : ROWS * (g + 1), :, :], in_=h_e[c][:, g, :])
@@ -172,7 +174,7 @@ def tile_rows_rnx_prod_kernel(tc, x, w, xb, hs, wo, bo, out):
         first_product(1, [POOL_GROUP])
         fuse_on_vector(0, first)
         move(0, first, nc.sync)
-        fuse_on_pool(1)
+        fuse_on_pool(1, LAST_ON_POOL)
         first_product(1, [first])
         fuse_on_vector(0, second)
         move(0, second, nc.sync)
@@ -184,6 +186,7 @@ def tile_rows_rnx_prod_kernel(tc, x, w, xb, hs, wo, bo, out):
         for g in (first, second):
             fuse_on_vector(1, g)
             move(1, g, nc.sync)
+        fuse_on_vector(1, POOL_GROUP, LAST_ON_POOL)
         move(1, POOL_GROUP, nc.scalar)
         fuse_on_vector(1, third)
         move(1, third, nc.sync)

from contextlib import ExitStack

import concourse.mybir as mybir

G, D, E, O, N = 4, 128, 128, 256, 512
FLOPS = 2 * G * D * E * N + 2 * G * E * O * N

F32 = mybir.dt.float32
BF16 = mybir.dt.bfloat16
U32 = mybir.dt.uint32
U8 = mybir.dt.uint8
FP8X4 = mybir.dt.float8_e4m3fn_x4
ACT = mybir.ActivationFunctionType
ALU = mybir.AluOpType

P = 128
PACK = 4
ROWS = 32
MM_N = 128
HALF = N // 2
OUT_TILES = O // P

POOL_GROUP = 1
VECTOR_GROUPS = (2, 0, 3)
LAST_ON_POOL = 192
WO_ON_VECTOR = 176
H_LAST_ON_VECTOR = 192


def tile_rows_rnx_prod_kernel(tc, x, w, xb, hs, wo, bo, out):
    nc = tc.nc
    x_k = x.rearrange("g (p j) n -> (g p) j n", j=PACK)
    w_k = w.rearrange("g (p j) e -> (g p) j e", j=PACK)
    wo_k = wo.rearrange("g (p j) o -> (g p) j o", j=PACK)
    xb_e = xb.rearrange("g e n -> e g n")
    out_p = out.rearrange("(t p) n -> p t n", p=P)

    with ExitStack() as ctx:
        sb = ctx.enter_context(tc.tile_pool(name="sb", bufs=1))
        ps = ctx.enter_context(tc.psum_pool(name="ps", bufs=1))
        ctx.enter_context(tc.manual_schedule())

        def tile(name, shape, dtype):
            return sb.tile(shape, dtype, name=name, align_bytes=64)

        def operand(name, width):
            return (
                tile(name + "_bf", [P, width, PACK], BF16),
                tile(name + "_codes", [P, width], U32),
                tile(name + "_scales", [P, width], U8),
            )

        w_raw = tile("w_raw", [P, PACK, E], F32)
        wo_raw = tile("wo_raw", [P, PACK, O], F32)
        vec_rows = tile("vec_rows", [P, ROWS], F32)
        vec = tile("vec", [P, ROWS], F32)
        x_pair = [tile("x_pair%d" % a, [P, 2, N], F32) for a in range(2)]
        xb_whole = [tile("xb_whole%d" % g, [P, N], F32) for g in range(2)]
        xb_half = [tile("xb_half%d" % c, [P, 2, HALF], F32) for c in range(2)]
        h_e = [tile("h_e%d" % c, [P, G, HALF], BF16) for c in range(2)]
        h_k = [tile("h_k%d" % c, [P, PACK, HALF], BF16) for c in range(2)]
        y = [tile("y%d" % c, [P, OUT_TILES, HALF], F32) for c in range(2)]
        z_scaled = [tile("z_scaled%d" % c, [P, HALF], F32) for c in range(2)]
        w_op = operand("w", E)
        wo_op = operand("wo", O)
        x_op = [operand("x%d" % c, HALF) for c in range(2)]
        h_op = [operand("h%d" % c, HALF) for c in range(2)]
        z = [ps.tile([P, N], F32, name="z%d" % g) for g in range(G)]
        u = [ps.tile([P, HALF], F32, name="u%d" % i) for i in range(2 * OUT_TILES)]

        def cols(c):
            return slice(c * HALF, (c + 1) * HALF)

        def xb_of(c, g):
            return xb_whole[g // 2][:, cols(c)] if g % 2 else xb_half[c][:, g // 2, :]

        def hs_of(g):
            return vec[:, 8 * g : 8 * g + 1]

        def bo_of(t):
            return vec[:, 16 * t + 1 : 16 * t + 2]

        def interleave(copy, into, rows):
            copy(out=into.rearrange("p (c i) j -> p c j i", i=4), in_=rows.rearrange("p j (c i) -> p c j i", i=4))

        def interleave_op(copy, op, raw, lo, hi):
            interleave(copy, op[0][:, lo:hi, :], raw[:, :, lo:hi])

        def interleave_x(copy, a, c, lo, hi):
            interleave(copy, x_op[c][0][:, lo:hi, 2 * a : 2 * a + 2], x_pair[a][:, :, c * HALF + lo : c * HALF + hi])

        def quantize(op, lo, hi):
            bf, codes, scales = op
            nc.vector.quantize_mx(
                out=codes[:, lo:hi].bitcast(FP8X4),
                scales=scales[:, lo:hi],
                in_=bf[:, lo:hi, :].rearrange("p n j -> p (n j)"),
            )

        def mx_product(acc, parts, stationary, m0, moving, n0):
            nc.tensor.matmul_mx(
                out=acc,
                lhsT=stationary[1][parts, m0 : m0 + P].bitcast(FP8X4),
                lhsT_scale=stationary[2][parts, m0 : m0 + P],
                rhs=moving[1][parts, n0 : n0 + MM_N].bitcast(FP8X4),
                rhs_scale=moving[2][parts, n0 : n0 + MM_N],
                start=True,
                stop=True,
            )

        def first_product(c, groups, starts=(0, MM_N)):
            for g in groups:
                for n0 in starts:
                    acc = z[g][:, c * HALF + n0 : c * HALF + n0 + MM_N]
                    mx_product(acc, slice(ROWS * g, ROWS * (g + 1)), w_op, 0, x_op[c], n0)

        def second_product(c, n0, accs):
            for t in range(OUT_TILES):
                mx_product(accs[t], slice(0, P), wo_op, t * P, h_op[c], n0)

        def fuse_on_vector(c, g, lo=0):
            nc.vector.scalar_tensor_tensor(
                out=h_e[c][:, g, lo:], in0=z[g][:, cols(c)][:, lo:], scalar=hs_of(g), in1=xb_of(c, g)[:, lo:],
                op0=ALU.mult, op1=ALU.mult,
            )

        def fuse_on_pool(c, hi=HALF):
            g = POOL_GROUP
            scaled = z_scaled[c][:, :hi]
            nc.scalar.activation(out=scaled, in_=z[g][:, cols(c)][:, :hi], func=ACT.Copy, scale=hs_of(g))
            nc.gpsimd.tensor_tensor(out=h_e[c][:, g, :hi], in0=scaled, in1=xb_of(c, g)[:, :hi], op=ALU.mult)

        def move(c, g, queue):
            queue.dma_start(out=h_k[c][ROWS * g : ROWS * (g + 1), :, :], in_=h_e[c][:, g, :])

        def tanh(c, t, lo, hi, acc):
            nc.scalar.activation(out=y[c][:, t, lo:hi], in_=acc, func=ACT.Tanh, bias=bo_of(t))

        def store(c, t, lo, hi):
            nc.sync.dma_start(out=out_p[:, t, c * HALF + lo : c * HALF + hi], in_=y[c][:, t, lo:hi])

        on_vector, on_scalar = nc.vector.tensor_copy, nc.scalar.copy
        first, second, third = VECTOR_GROUPS

        nc.vector.memset(vec_rows[:], 0.0)
        nc.sync.dma_start(out=x_pair[0][:], in_=x_k[:, 0:2, :])
        nc.sync.dma_start(out=w_raw[:], in_=w_k)
        nc.sync.dma_start(out=vec_rows[0:P:8, :], in_=hs.rearrange("g (q i) o -> q g (i o)", i=ROWS))
        nc.sync.dma_start(out=vec_rows[1:P:16, :], in_=bo.rearrange("(t q i) o -> q t (i o)", t=OUT_TILES, i=ROWS))
        nc.sync.dma_start(out=x_pair[1][:], in_=x_k[:, 2:4, :])
        nc.sync.dma_start(out=xb_whole[0][:], in_=xb_e[:, 1, :])
        nc.sync.dma_start(out=xb_half[0][:], in_=xb_e[:, 0:3:2, cols(0)])
        nc.sync.dma_start(out=xb_whole[1][:], in_=xb_e[:, 3, :])
        for g in (2, 0):
            nc.sync.dma_start(out=xb_half[1][:, g // 2, :], in_=xb_e[:, g, cols(1)])
        nc.sync.dma_start(out=wo_raw[:], in_=wo_k)

        interleave_x(on_vector, 0, 0, 0, HALF)
        interleave_x(on_scalar, 0, 1, 0, HALF)
        interleave_op(on_vector, w_op, w_raw, 0, E)
        nc.vector.transpose(out=vec[:], in_=vec_rows[:])
        quantize(w_op, 0, E)

        for c in range(2):
            interleave_x(on_vector, 1, c, 0, MM_N)
            interleave_x(on_scalar, 1, c, MM_N, HALF)
        for n0 in (0, MM_N):
            quantize(x_op[0], n0, n0 + MM_N)
            first_product(0, [POOL_GROUP, first], [n0])
        first_product(0, [second, third])
        quantize(x_op[1], 0, HALF)

        fuse_on_pool(0)
        first_product(1, [POOL_GROUP])
        fuse_on_vector(0, first)
        move(0, first, nc.sync)
        fuse_on_pool(1, LAST_ON_POOL)
        first_product(1, [first])
        fuse_on_vector(0, second)
        move(0, second, nc.sync)
        first_product(1, [second])
        fuse_on_vector(0, third)
        move(0, third, nc.sync)
        move(0, POOL_GROUP, nc.sync)
        first_product(1, [third])
        for g in (first, second):
            fuse_on_vector(1, g)
            move(1, g, nc.sync)
        fuse_on_vector(1, POOL_GROUP, LAST_ON_POOL)
        move(1, POOL_GROUP, nc.scalar)
        fuse_on_vector(1, third)
        move(1, third, nc.sync)

        interleave_op(on_vector, wo_op, wo_raw, 0, WO_ON_VECTOR)
        interleave_op(on_scalar, wo_op, wo_raw, WO_ON_VECTOR, O)
        interleave_op(on_vector, h_op[0], h_k[0], 0, MM_N)
        interleave_op(on_scalar, h_op[0], h_k[0], MM_N, HALF)
        quantize(wo_op, 0, O)
        for n0 in (0, MM_N):
            quantize(h_op[0], n0, n0 + MM_N)
            second_product(0, n0, [u[t][:, n0 : n0 + MM_N] for t in range(OUT_TILES)])

        interleave_op(on_vector, h_op[1], h_k[1], 0, MM_N)
        interleave_op(on_scalar, h_op[1], h_k[1], H_LAST_ON_VECTOR, HALF)
        interleave_op(on_vector, h_op[1], h_k[1], MM_N, H_LAST_ON_VECTOR)
        for t in range(OUT_TILES):
            tanh(0, t, 0, HALF, u[t][:])
            store(0, t, 0, HALF)
        early = [u[OUT_TILES + t][:, 0:MM_N] for t in range(OUT_TILES)]
        late = [u[t][:, 0:MM_N] for t in range(OUT_TILES)]
        quantize(h_op[1], 0, MM_N)
        second_product(1, 0, early)
        quantize(h_op[1], MM_N, HALF)
        second_product(1, MM_N, late)
        for t in range(OUT_TILES):
            tanh(1, t, 0, MM_N, early[t])
        store(1, slice(0, OUT_TILES), 0, MM_N)
        for t in range(OUT_TILES):
            tanh(1, t, MM_N, HALF, late[t])
            store(1, t, MM_N, HALF)
